import numpy as np
import ml_dtypes


def mxq(x, axis, fmt="e4m3"):
    dtype, down = {"e4m3": (ml_dtypes.float8_e4m3fn, 7), "e5m2": (ml_dtypes.float8_e5m2, 14)}[fmt]
    v = np.moveaxis(np.asarray(x, np.float32).astype(ml_dtypes.bfloat16).astype(np.float64), axis, -1)
    blocks = v.reshape(v.shape[:-1] + (-1, 32))
    amax = np.abs(blocks).max(-1, keepdims=True)
    byte = np.maximum(np.where(amax > 0, np.frexp(amax)[1] - 1 + 127, 0) - down, 1)
    scale = np.exp2(byte - 127.0)
    codes = (blocks / scale).astype(np.float32).astype(dtype).astype(np.float64)
    return np.moveaxis((codes * scale).reshape(v.shape), -1, axis)


WIDE = False


def mx_kscale(k):
    if not WIDE:
        return np.ones(k)
    levels = np.array([10, -10, 5, -5, 0])
    if k % 512:
        return np.exp2(np.random.permutation(np.resize(levels, k // 32))).repeat(32)
    a = np.empty((k // 512, 16))
    for p in range(k // 512):
        a[p, :8] = np.random.permutation(np.resize(levels, 8))
        for g in range(8):
            far = levels[np.abs(levels - a[p, g]) >= 10]
            a[p, g + 8] = far[np.random.randint(len(far))]
    return np.exp2(a.ravel()).repeat(32)


def f64(x):
    return np.asarray(x).astype(np.float64)


def striped(idx):
    return np.tile(idx.reshape(-1, 16).T, (8, 1)).astype(np.uint16)


def unstriped(offs):
    return offs[:16].T.reshape(-1).astype(np.int64)


def pack_weight(w):
    k, n = w.shape
    w = f64(np.asarray(w, np.float32).astype(ml_dtypes.bfloat16)).reshape(k // 32, 32, n)
    amax = np.abs(w).max(1)
    byte = np.clip(np.where(amax > 0, np.frexp(amax)[1] - 1 + 127 - 7, 1), 1, 254)
    scaled = (w * np.exp2(127.0 - byte)[:, None, :]).reshape(k, n).astype(np.float32)
    words = np.ascontiguousarray(scaled.reshape(k // 512, 128, 4, n).transpose(0, 1, 3, 2)).astype(ml_dtypes.float8_e4m3fn).view(np.uint8)
    return words, np.ascontiguousarray(byte.astype(np.uint8).reshape(k // 512, 16, n))


def unpack_weight(words, scales):
    g, p, n, _ = words.shape
    vals = np.ascontiguousarray(words).view(ml_dtypes.float8_e4m3fn).astype(np.float64) * np.repeat(np.exp2(scales.astype(np.float64) - 127.0), 8, axis=1)[..., None]
    return vals.transpose(0, 1, 3, 2).reshape(g * 512, n)


K, T, S, D, N, H, V, U = 512, 2048, 1024, 4, 128, 512, 256, 512


def setup_inputs():
    n = np.random.standard_normal
    s = mx_kscale(K)[:, None]
    u = mx_kscale(H)
    packed_xT = pack_weight(n((K, T)) * s)
    return {
        "x_words": packed_xT[0],
        "x_scales": packed_xT[1],
        "w1": (n((K, H)) / np.sqrt(K) / s).astype(np.float32),
        "w2": (n((K, H)) / np.sqrt(K) / s).astype(np.float32),
        "clm": (n((H, U))).astype(np.float32),
        "unit": (np.random.uniform(0.6, 1.4, (H, 1)) * u[:, None]).astype(np.float32),
        "w3": (n((H, N)) / np.sqrt(H) / u[:, None]).astype(np.float32),
        "offs": striped(np.random.permutation(T)[:S]),
        "prv": striped(np.random.permutation(S)),
        "path": striped(np.random.permutation(np.concatenate([np.arange(V), np.random.randint(0, V, U - V)]))),
    }


def reference(x_words, x_scales, w1, w2, clm, unit, w3, offs, prv, path):
    xq = unpack_weight(x_words, x_scales)[:, unstriped(offs)]
    dl = mxq(f64(w1), 0, "e4m3").T @ xq
    pos = np.tanh(dl)
    ds = mxq(f64(w2), 0, "e4m3").T @ xq
    dp = pos[:, unstriped(prv)]
    trd = np.abs(pos - dp)
    pnl = pos * ds - (0.4 * trd)
    term = pnl.reshape(len(pnl), -1, D).sum(axis=2)
    tpp = term[:, unstriped(path)]
    net = tpp - f64(clm)
    eu = np.exp(-1.0 * np.tanh(net))
    hid = f64(unit) * eu
    return mxq(f64(w3), 0, "e4m3").T @ mxq(hid, 0, "e4m3")

@@ -1,0 +1,258 @@
+from contextlib import ExitStack
+
+import concourse.mybir as mybir
+from concourse.masks import make_identity
+
+F32 = mybir.dt.float32
+BF16 = mybir.dt.bfloat16
+I32 = mybir.dt.int32
+U32 = mybir.dt.uint32
+U16 = mybir.dt.uint16
+U8 = mybir.dt.uint8
+FP8X4 = mybir.dt.float8_e4m3fn_x4
+ACT = mybir.ActivationFunctionType
+ALU = mybir.AluOpType
+AX = mybir.AxisListType
+
+P = 128
+K, T, S, D, N, H, V, U = 512, 2048, 1024, 4, 128, 512, 256, 512
+HALF = 512
+CH = 256
+FLOPS = 2 * K * H * S * 2 + 2 * H * N * U
+
+PATH_ON_SCALAR = ()
+PRV_ON_SCALAR = ((1, 0), (1, 1))
+REDUCE_ON_VECTOR = ()
+EVAC_ON_VECTOR = ()
+DL_BUFS = 3
+DS_BUFS = 2
+RING = 8
+LAST_STEPPED = 1
+TAIL = 4
+W1_SPLIT = 1
+SKEW = (0, 3, 2, 2, 4, 7, 8, 8)
+RES_V = 0
+
+
+def tile_picked_ydeepm_ent_p_kernel(tc, x_words, x_scales, w1, w2, clm, unit, w3, offs, prv, path, out):
+    nc = tc.nc
+    with ExitStack() as ctx:
+        keep = ctx.enter_context(tc.tile_pool(name="keep", bufs=1))
+        ring = ctx.enter_context(tc.tile_pool(name="ring", bufs=RING))
+        psum = ctx.enter_context(tc.psum_pool(name="psum", bufs=1))
+
+        offs_t = keep.tile([P, S // 16], U16, name="offs_t")
+        prv_t = keep.tile([P, S // 16], U16, name="prv_t")
+        path_t = keep.tile([P, U // 16], U16, name="path_t")
+        xw = keep.tile([P, T], U32, name="xw", align_bytes=64)
+        xs = keep.tile([P, T], U8, name="xs", align_bytes=64)
+        w1_cols = H // (1 + W1_SPLIT)
+        w1_raw = [keep.tile([P, 4, w1_cols], F32, name="w1_raw%d" % b) for b in range(1 + W1_SPLIT)]
+        w2_raw = keep.tile([P, 4, H], F32, name="w2_raw")
+        w3_raw = keep.tile([P, 4, N], F32, name="w3_raw")
+        clm_t = keep.tile([P, 4, U], F32, name="clm_t")
+        unit_t = keep.tile([P, 4], F32, name="unit_t")
+        ident = keep.tile([P, P], F32, name="ident")
+
+        nc.sync.dma_start(offs_t[:], offs)
+        for q in range(4):
+            nc.sync.dma_start(xs[32 * q : 32 * q + 32, :].bitcast(I32), x_scales[0, 4 * q : 4 * q + 4, :].bitcast(I32).partition_broadcast(8))
+        nc.sync.dma_start(xw[:].bitcast(I32), x_words[0].rearrange("p n r -> p (n r)").bitcast(I32))
+        for b in range(1 + W1_SPLIT):
+            nc.sync.dma_start(w1_raw[b][:], w1.rearrange("(p j) c -> p j c", j=4)[:, :, w1_cols * b : w1_cols * (b + 1)])
+        nc.sync.dma_start(w2_raw[:], w2.rearrange("(p j) c -> p j c", j=4))
+        nc.sync.dma_start(prv_t[:], prv)
+        nc.sync.dma_start(w3_raw[:], w3.rearrange("(p j) c -> p j c", j=4))
+        nc.sync.dma_start(path_t[:], path)
+        nc.sync.dma_start(unit_t[:], unit.rearrange("(p t) o -> p (t o)", t=4))
+        nc.sync.dma_start(clm_t[:], clm.rearrange("(p t) r -> p t r", t=4))
+        make_identity(nc, ident[:])
+
+        gs = keep.tile([P, S], U8, name="gs", align_bytes=64)
+        nc.vector.tensor_copy(gs[:], xs[:].indirect(offs_t[:]))
+
+        def deal(wb, raw, a, m0, on_scalar):
+            src = raw[:].rearrange("p j (m t) -> p m j t", t=4)[:, :, :, 2 * a : 2 * a + 2]
+            dst = wb[:].rearrange("p (t m j) -> p m j t", t=2, j=4)[:, m0 : m0 + src.shape[1]]
+            if on_scalar:
+                nc.scalar.copy(dst, src)
+            else:
+                nc.vector.tensor_copy(dst, src)
+
+        def quantise(src, width, name):
+            codes = keep.tile([P, width], U32, name=name + "_c", align_bytes=64)
+            scales = keep.tile([P, width], U8, name=name + "_s", align_bytes=64)
+            nc.vector.quantize_mx(out=codes[:].bitcast(FP8X4), scales=scales[:], in_=src)
+            return codes, scales
+
+        gw = [keep.tile([P, HALF], U32, name="gw%d" % h, align_bytes=64) for h in range(2)]
+        for h in range(2):
+            nc.vector.tensor_copy(gw[h][:], xw[:].indirect(offs_t[:, 32 * h : 32 * h + 32]))
+
+        w1b = [keep.tile([P, 1024], BF16, name="w1b%d" % a, align_bytes=64) for a in range(2)]
+        w2b = [keep.tile([P, 1024], BF16, name="w2b%d" % a, align_bytes=64) for a in range(2)]
+        if W1_SPLIT:
+            deal(w1b[0], w1_raw[0], 0, 0, True)
+            deal(w1b[1], w1_raw[0], 1, 0, True)
+            deal(w1b[0], w1_raw[1], 0, 64, False)
+            deal(w1b[1], w1_raw[1], 1, 64, True)
+        else:
+            deal(w1b[0], w1_raw[0], 0, 0, False)
+            deal(w1b[1], w1_raw[0], 1, 0, True)
+        w1q = [quantise(w1b[a][:], 256, "w1q%d" % a) for a in range(2)]
+        w2q = []
+        for a in range(2):
+            deal(w2b[a], w2_raw, a, 0, False)
+            w2q.append(quantise(w2b[a][:], 256, "w2q%d" % a))
+        w3b = keep.tile([P, N, 4], BF16, name="w3b", align_bytes=64)
+        nc.vector.tensor_copy(w3b[:].rearrange("p (c i) j -> p c j i", i=4), w3_raw[:].rearrange("p j (c i) -> p c j i", i=4))
+        w3c, w3s = quantise(w3b[:].rearrange("p n j -> p (n j)"), N, "w3q")
+
+        def product(wq, t, h, bank):
+            codes, scales = wq[t // 2]
+            cols = slice(P * (t % 2), P * (t % 2) + P)
+            nc.tensor.matmul_mx(
+                out=bank[:],
+                lhsT=codes[:, cols].bitcast(FP8X4),
+                lhsT_scale=scales[:, cols],
+                rhs=gw[h][:].bitcast(FP8X4),
+                rhs_scale=gs[:, HALF * h : HALF * h + HALF],
+                start=True,
+                stop=True,
+            )
+
+        pos = [keep.tile([P, S], F32, name="pos%d" % t) for t in range(4)]
+        term = [keep.tile([P, 2 * V], F32, name="term%d" % t) for t in range(4)]
+        hb = keep.tile([P, 4, U], BF16, name="hb")
+        hq = keep.tile([P, U, 4], BF16, name="hq", align_bytes=64)
+        twin, loss, diff, cost, back, spent, net, eu = {}, {}, {}, {}, {}, {}, {}, {}
+
+        def half(h):
+            return slice(HALF * h, HALF * h + HALF)
+
+        def chunks(t, c):
+            n = TAIL // 2 if t == 3 else 1
+            w = CH // n
+            return [slice(CH * c + w * k, CH * c + w * k + w) for k in range(n)]
+
+        def leave(t, dst, bank):
+            if t in EVAC_ON_VECTOR:
+                nc.vector.tensor_copy(dst, bank)
+            else:
+                nc.scalar.copy(dst, bank)
+
+        def position(t, h):
+            bank = psum.tile([P, HALF], F32, name="dl", tag="dl", bufs=DL_BUFS)
+            product(w1q, t, h, bank)
+            nc.scalar.activation(pos[t][:, half(h)], bank[:], ACT.Tanh)
+            if (t, h) not in PRV_ON_SCALAR:
+                twin[t, h] = keep.tile([P, HALF], F32, name="twin%d_%d" % (t, h))
+                nc.sync.dma_start(twin[t, h][:], pos[t][:, half(h)])
+
+        def moves(t, h):
+            bank = psum.tile([P, HALF], F32, name="ds", tag="ds", bufs=DS_BUFS)
+            product(w2q, t, h, bank)
+            loss[t, h] = ring.tile([P, D, P], F32, name="loss")
+            nc.vector.scalar_tensor_tensor(
+                loss[t, h][:].rearrange("p d v -> p v d"),
+                bank[:].rearrange("p (v d) -> p v d", d=D),
+                -1.0,
+                pos[t][:, half(h)].rearrange("p (v d) -> p v d", d=D),
+                ALU.mult,
+                ALU.mult,
+            )
+
+        def trades(t, h):
+            diff[t, h] = ring.tile([P, HALF], F32, name="diff")
+            looked = pos[t][:].indirect(prv_t[:, 32 * h : 32 * h + 32])
+            if (t, h) in PRV_ON_SCALAR:
+                dp = ring.tile([P, HALF], F32, name="dp")
+                nc.scalar.activation(dp[:], looked, ACT.Copy)
+                nc.vector.tensor_tensor(diff[t, h][:], dp[:], pos[t][:, half(h)], ALU.subtract)
+            else:
+                nc.vector.tensor_tensor(diff[t, h][:], looked, twin[t, h][:], ALU.subtract)
+
+        def costs(t, h):
+            grouped = diff[t, h][:].rearrange("p (v d) -> p v d", d=D)
+            if t in REDUCE_ON_VECTOR:
+                if h == 0:
+                    spent[t] = keep.tile([P, V], F32, name="spent%d" % t)
+                nc.vector.tensor_reduce(spent[t][:, P * h : P * h + P], grouped, AX.X, ALU.add, apply_absolute_value=True)
+            else:
+                cost[t, h] = ring.tile([P, D, P], F32, name="cost")
+                nc.scalar.activation(cost[t, h][:].rearrange("p d v -> p v d"), grouped, ACT.Abs, scale=0.4)
+
+        def sums(t, h):
+            parts = [loss[t, h][:, d, :] for d in range(D)]
+            if t not in REDUCE_ON_VECTOR:
+                parts = parts + [cost[t, h][:, d, :] for d in range(D)]
+            bank = psum.tile([P, P], F32, name="sums", tag="sums", bufs=2)
+            for n, part in enumerate(parts):
+                nc.tensor.matmul(bank[:], lhsT=part, rhs=ident[:], is_transpose=True, start=(n == 0), stop=(n == len(parts) - 1))
+            turned = term[t][:, V + P * h : V + P * h + P]
+            leave(t, turned, bank[:])
+            if h == 0:
+                back[t] = psum.tile([P, V], F32, name="back", tag="back", bufs=1)
+            nc.tensor.transpose(back[t][:, P * h : P * h + P], turned, ident[:])
+            if h == 1:
+                if t in REDUCE_ON_VECTOR:
+                    nc.vector.scalar_tensor_tensor(term[t][:, 0:V], spent[t][:], 0.4, back[t][:], ALU.mult, ALU.add)
+                else:
+                    leave(t, term[t][:, 0:V], back[t][:])
+
+        def lookup(t, c):
+            net[t, c] = ring.tile([P, CH], F32, name="net")
+            for cols in chunks(t, c):
+                mine = slice(cols.start - CH * c, cols.stop - CH * c)
+                looked = term[t][:].indirect(path_t[:, cols.start // 16 : cols.stop // 16])
+                if t in PATH_ON_SCALAR:
+                    tpp = ring.tile([P, CH], F32, name="tpp")
+                    nc.scalar.activation(tpp[:, mine], looked, ACT.Copy)
+                    nc.vector.tensor_tensor(net[t, c][:, mine], tpp[:, mine], clm_t[:, t, cols], ALU.add)
+                else:
+                    nc.vector.tensor_tensor(net[t, c][:, mine], looked, clm_t[:, t, cols], ALU.add)
+
+        def utility(t, c):
+            th = ring.tile([P, CH], F32, name="th")
+            eu[t, c] = ring.tile([P, CH], F32, name="eu")
+            for cols in chunks(t, c):
+                mine = slice(cols.start - CH * c, cols.stop - CH * c)
+                nc.scalar.activation(th[:, mine], net[t, c][:, mine], ACT.Tanh)
+                nc.scalar.activation(eu[t, c][:, mine], th[:, mine], ACT.Exp)
+
+        def weave(cols, tiles):
+            nc.vector.tensor_copy(
+                hq[:, cols, 0:tiles].rearrange("p (c i) t -> p c t i", i=4), hb[:, 0:tiles, cols].rearrange("p t (c i) -> p c t i", i=4)
+            )
+
+        def hidden(t, c):
+            for cols in chunks(t, c):
+                mine = slice(cols.start - CH * c, cols.stop - CH * c)
+                if LAST_STEPPED and t == 3:
+                    nc.vector.tensor_scalar(hq[:, cols, t], eu[t, c][:, mine], unit_t[:, t : t + 1], None, ALU.mult)
+                else:
+                    nc.vector.tensor_scalar(hb[:, t, cols], eu[t, c][:, mine], unit_t[:, t : t + 1], None, ALU.mult)
+                if LAST_STEPPED and t == 2:
+                    weave(cols, 3)
+                if t == 3:
+                    if not LAST_STEPPED:
+                        weave(cols, 4)
+                    w = cols.stop - cols.start
+                    hc, hs = quantise(hq[:, cols, :].rearrange("p r t -> p (r t)"), w, "hq%d" % cols.start)
+                    bank = psum.tile([P, HALF], F32, name="dl", tag="dl", bufs=DL_BUFS)
+                    nc.tensor.matmul_mx(
+                        out=bank[:, 0:w], lhsT=w3c[:].bitcast(FP8X4), lhsT_scale=w3s[:], rhs=hc[:].bitcast(FP8X4), rhs_scale=hs[:], start=True, stop=True
+                    )
+                    res = keep.tile([P, w], F32, name="res%d" % cols.start)
+                    if RES_V and cols.stop == U:
+                        nc.vector.tensor_copy(res[:], bank[:, 0:w])
+                    else:
+                        nc.scalar.copy(res[:], bank[:, 0:w])
+                    nc.sync.dma_start(out[:, cols], res[:])
+
+        stages = (position, moves, trades, costs, sums, lookup, utility, hidden)
+        for step in range(8 + max(SKEW)):
+            for n, stage in enumerate(stages):
+                unit_no = step - SKEW[n]
+                if 0 <= unit_no < 8:
+                    stage(unit_no // 2, unit_no % 2)

@@ -1,7 +1,6 @@
 from contextlib import ExitStack
 
 import concourse.mybir as mybir
-from concourse.masks import make_identity
 
 F32 = mybir.dt.float32
 BF16 = mybir.dt.bfloat16
@@ -20,18 +19,24 @@ HALF = 512
 CH = 256
 FLOPS = 2 * K * H * S * 2 + 2 * H * N * U
 
-PATH_ON_SCALAR = ()
-PRV_ON_SCALAR = ((1, 0), (1, 1))
-REDUCE_ON_VECTOR = ()
+PATH_ON_SCALAR = (1, 2)
+PRV_ON_SCALAR = ((0, 0), (0, 1), (1, 0), (1, 1), (2, 0), (2, 1), (3, 0), (3, 1))
+MODE = "NNNN"
 EVAC_ON_VECTOR = ()
-DL_BUFS = 3
+DL_BUFS = 2
 DS_BUFS = 2
-RING = 8
+RING = 4
 LAST_STEPPED = 1
 TAIL = 4
 W1_SPLIT = 1
-SKEW = (0, 3, 2, 2, 4, 7, 8, 8)
+SKEW = (0, 1, 3, 3, 3, 6, 6, 7)
 RES_V = 0
+WIDE = (0, 1)
+W3_ON_SCALAR = 0
+W2B_ON_SCALAR = 0
+PER_TILE = 1
+W3_STEP = 2
+SCALE_ON_SCALAR = (0, 1, 2)
 
 
 def tile_picked_ydeepm_ent_p_kernel(tc, x_words, x_scales, w1, w2, clm, unit, w3, offs, prv, path, out):
@@ -52,7 +57,6 @@ def tile_picked_ydeepm_ent_p_kernel(tc, x_words, x_scales, w1, w2, clm, unit, w3
         w3_raw = keep.tile([P, 4, N], F32, name="w3_raw")
         clm_t = keep.tile([P, 4, U], F32, name="clm_t")
         unit_t = keep.tile([P, 4], F32, name="unit_t")
-        ident = keep.tile([P, P], F32, name="ident")
 
         nc.sync.dma_start(offs_t[:], offs)
         for q in range(4):
@@ -66,7 +70,6 @@ def tile_picked_ydeepm_ent_p_kernel(tc, x_words, x_scales, w1, w2, clm, unit, w3
         nc.sync.dma_start(path_t[:], path)
         nc.sync.dma_start(unit_t[:], unit.rearrange("(p t) o -> p (t o)", t=4))
         nc.sync.dma_start(clm_t[:], clm.rearrange("(p t) r -> p t r", t=4))
-        make_identity(nc, ident[:])
 
         gs = keep.tile([P, S], U8, name="gs", align_bytes=64)
         nc.vector.tensor_copy(gs[:], xs[:].indirect(offs_t[:]))
@@ -102,11 +105,19 @@ def tile_picked_ydeepm_ent_p_kernel(tc, x_words, x_scales, w1, w2, clm, unit, w3
         w1q = [quantise(w1b[a][:], 256, "w1q%d" % a) for a in range(2)]
         w2q = []
         for a in range(2):
-            deal(w2b[a], w2_raw, a, 0, False)
+            deal(w2b[a], w2_raw, a, 0, a == 1 and W2B_ON_SCALAR)
             w2q.append(quantise(w2b[a][:], 256, "w2q%d" % a))
         w3b = keep.tile([P, N, 4], BF16, name="w3b", align_bytes=64)
-        nc.vector.tensor_copy(w3b[:].rearrange("p (c i) j -> p c j i", i=4), w3_raw[:].rearrange("p j (c i) -> p c j i", i=4))
-        w3c, w3s = quantise(w3b[:].rearrange("p n j -> p (n j)"), N, "w3q")
+        w3q = []
+
+        def last_weights():
+            dst = w3b[:].rearrange("p (c i) j -> p c j i", i=4)
+            src = w3_raw[:].rearrange("p j (c i) -> p c j i", i=4)
+            if W3_ON_SCALAR:
+                nc.scalar.copy(dst, src)
+            else:
+                nc.vector.tensor_copy(dst, src)
+            w3q.extend(quantise(w3b[:].rearrange("p n j -> p (n j)"), N, "w3q"))
 
         def product(wq, t, h, bank):
             codes, scales = wq[t // 2]
@@ -122,15 +133,17 @@ def tile_picked_ydeepm_ent_p_kernel(tc, x_words, x_scales, w1, w2, clm, unit, w3
             )
 
         pos = [keep.tile([P, S], F32, name="pos%d" % t) for t in range(4)]
-        term = [keep.tile([P, 2 * V], F32, name="term%d" % t) for t in range(4)]
+        term = [keep.tile([P, 3 * V if MODE[t] in "NA" else 2 * V], F32, name="term%d" % t) for t in range(4)]
         hb = keep.tile([P, 4, U], BF16, name="hb")
         hq = keep.tile([P, U, 4], BF16, name="hq", align_bytes=64)
-        twin, loss, diff, cost, back, spent, net, eu = {}, {}, {}, {}, {}, {}, {}, {}
+        twin, loss, diff, cost, back, spent, net, eu, th, tpp = {}, {}, {}, {}, {}, {}, {}, {}, {}, {}
 
         def half(h):
             return slice(HALF * h, HALF * h + HALF)
 
         def chunks(t, c):
+            if t in WIDE and MODE[t] in "NA":
+                return [slice(0, U)] if c == 0 else []
             n = TAIL // 2 if t == 3 else 1
             w = CH // n
             return [slice(CH * c + w * k, CH * c + w * k + w) for k in range(n)]
@@ -152,6 +165,10 @@ def tile_picked_ydeepm_ent_p_kernel(tc, x_words, x_scales, w1, w2, clm, unit, w3
         def moves(t, h):
             bank = psum.tile([P, HALF], F32, name="ds", tag="ds", bufs=DS_BUFS)
             product(w2q, t, h, bank)
+            if MODE[t] in "NA":
+                loss[t, h] = ring.tile([P, HALF], F32, name="loss")
+                nc.vector.scalar_tensor_tensor(loss[t, h][:], bank[:], -1.0, pos[t][:, half(h)], ALU.mult, ALU.mult)
+                return
             loss[t, h] = ring.tile([P, D, P], F32, name="loss")
             nc.vector.scalar_tensor_tensor(
                 loss[t, h][:].rearrange("p d v -> p v d"),
@@ -174,7 +191,10 @@ def tile_picked_ydeepm_ent_p_kernel(tc, x_words, x_scales, w1, w2, clm, unit, w3
 
         def costs(t, h):
             grouped = diff[t, h][:].rearrange("p (v d) -> p v d", d=D)
-            if t in REDUCE_ON_VECTOR:
+            if MODE[t] == "A":
+                cost[t, h] = ring.tile([P, HALF], F32, name="cost")
+                nc.scalar.activation(cost[t, h][:], diff[t, h][:], ACT.Abs, scale=0.4)
+            elif MODE[t] in "RN":
                 if h == 0:
                     spent[t] = keep.tile([P, V], F32, name="spent%d" % t)
                 nc.vector.tensor_reduce(spent[t][:, P * h : P * h + P], grouped, AX.X, ALU.add, apply_absolute_value=True)
@@ -183,42 +203,60 @@ def tile_picked_ydeepm_ent_p_kernel(tc, x_words, x_scales, w1, w2, clm, unit, w3
                 nc.scalar.activation(cost[t, h][:].rearrange("p d v -> p v d"), grouped, ACT.Abs, scale=0.4)
 
         def sums(t, h):
+            if MODE[t] in "NA":
+                src = loss[t, h]
+                if MODE[t] == "A":
+                    src = ring.tile([P, HALF], F32, name="pnl")
+                    nc.vector.tensor_tensor(src[:], loss[t, h][:], cost[t, h][:], ALU.add)
+                grouped = src[:].rearrange("p (v d) -> p v d", d=D)
+                pairs = term[t][:, V : 3 * V].rearrange("p (v e) -> p v e", e=2)
+                nc.vector.tensor_tensor(pairs[:, P * h : P * h + P, :], grouped[:, :, 0:2], grouped[:, :, 2:4], ALU.add)
+                if PER_TILE and h == 0:
+                    return
+                vs = slice(0, V) if PER_TILE else slice(P * h, P * h + P)
+                first = pairs[:, vs, 0]
+                if MODE[t] == "N":
+                    part = ring.tile([P, V], F32, name="part")
+                    nc.vector.scalar_tensor_tensor(part[:, vs], spent[t][:, vs], 0.4, first, ALU.mult, ALU.add)
+                    first = part[:, vs]
+                nc.vector.tensor_tensor(term[t][:, vs], first, pairs[:, vs, 1], ALU.add)
+                return
             parts = [loss[t, h][:, d, :] for d in range(D)]
-            if t not in REDUCE_ON_VECTOR:
+            if MODE[t] == "P":
                 parts = parts + [cost[t, h][:, d, :] for d in range(D)]
             bank = psum.tile([P, P], F32, name="sums", tag="sums", bufs=2)
             for n, part in enumerate(parts):
-                nc.tensor.matmul(bank[:], lhsT=part, rhs=ident[:], is_transpose=True, start=(n == 0), stop=(n == len(parts) - 1))
+                nc.tensor.matmul(bank[:], lhsT=part, rhs=None, is_transpose=True, start=(n == 0), stop=(n == len(parts) - 1))
             turned = term[t][:, V + P * h : V + P * h + P]
             leave(t, turned, bank[:])
             if h == 0:
                 back[t] = psum.tile([P, V], F32, name="back", tag="back", bufs=1)
-            nc.tensor.transpose(back[t][:, P * h : P * h + P], turned, ident[:])
+            nc.tensor.transpose(back[t][:, P * h : P * h + P], turned, None)
             if h == 1:
-                if t in REDUCE_ON_VECTOR:
+                if MODE[t] == "R":
                     nc.vector.scalar_tensor_tensor(term[t][:, 0:V], spent[t][:], 0.4, back[t][:], ALU.mult, ALU.add)
                 else:
                     leave(t, term[t][:, 0:V], back[t][:])
 
         def lookup(t, c):
-            net[t, c] = ring.tile([P, CH], F32, name="net")
+            if c == 0:
+                net[t] = keep.tile([P, U], F32, name="net%d" % t)
+                tpp[t] = keep.tile([P, U], F32, name="tpp%d" % t)
             for cols in chunks(t, c):
-                mine = slice(cols.start - CH * c, cols.stop - CH * c)
                 looked = term[t][:].indirect(path_t[:, cols.start // 16 : cols.stop // 16])
                 if t in PATH_ON_SCALAR:
-                    tpp = ring.tile([P, CH], F32, name="tpp")
-                    nc.scalar.activation(tpp[:, mine], looked, ACT.Copy)
-                    nc.vector.tensor_tensor(net[t, c][:, mine], tpp[:, mine], clm_t[:, t, cols], ALU.add)
+                    nc.scalar.activation(tpp[t][:, cols], looked, ACT.Copy)
+                    nc.vector.tensor_tensor(net[t][:, cols], tpp[t][:, cols], clm_t[:, t, cols], ALU.add)
                 else:
-                    nc.vector.tensor_tensor(net[t, c][:, mine], looked, clm_t[:, t, cols], ALU.add)
+                    nc.vector.tensor_tensor(net[t][:, cols], looked, clm_t[:, t, cols], ALU.add)
 
         def utility(t, c):
-            th = ring.tile([P, CH], F32, name="th")
-            eu[t, c] = ring.tile([P, CH], F32, name="eu")
+            if c == 0:
+                th[t] = keep.tile([P, U], F32, name="th%d" % t)
+                eu[t] = keep.tile([P, U], F32, name="eu%d" % t)
             for cols in chunks(t, c):
-                mine = slice(cols.start - CH * c, cols.stop - CH * c)
-                nc.scalar.activation(th[:, mine], net[t, c][:, mine], ACT.Tanh)
-                nc.scalar.activation(eu[t, c][:, mine], th[:, mine], ACT.Exp)
+                nc.scalar.activation(th[t][:, cols], net[t][:, cols], ACT.Tanh)
+                nc.scalar.activation(eu[t][:, cols], th[t][:, cols], ACT.Exp)
 
         def weave(cols, tiles):
             nc.vector.tensor_copy(
@@ -227,11 +265,12 @@ def tile_picked_ydeepm_ent_p_kernel(tc, x_words, x_scales, w1, w2, clm, unit, w3
 
         def hidden(t, c):
             for cols in chunks(t, c):
-                mine = slice(cols.start - CH * c, cols.stop - CH * c)
                 if LAST_STEPPED and t == 3:
-                    nc.vector.tensor_scalar(hq[:, cols, t], eu[t, c][:, mine], unit_t[:, t : t + 1], None, ALU.mult)
+                    nc.vector.tensor_scalar(hq[:, cols, t], eu[t][:, cols], unit_t[:, t : t + 1], None, ALU.mult)
+                elif t in SCALE_ON_SCALAR:
+                    nc.scalar.activation(hb[:, t, cols], eu[t][:, cols], ACT.Copy, scale=unit_t[:, t : t + 1])
                 else:
-                    nc.vector.tensor_scalar(hb[:, t, cols], eu[t, c][:, mine], unit_t[:, t : t + 1], None, ALU.mult)
+                    nc.vector.tensor_scalar(hb[:, t, cols], eu[t][:, cols], unit_t[:, t : t + 1], None, ALU.mult)
                 if LAST_STEPPED and t == 2:
                     weave(cols, 3)
                 if t == 3:
@@ -241,7 +280,7 @@ def tile_picked_ydeepm_ent_p_kernel(tc, x_words, x_scales, w1, w2, clm, unit, w3
                     hc, hs = quantise(hq[:, cols, :].rearrange("p r t -> p (r t)"), w, "hq%d" % cols.start)
                     bank = psum.tile([P, HALF], F32, name="dl", tag="dl", bufs=DL_BUFS)
                     nc.tensor.matmul_mx(
-                        out=bank[:, 0:w], lhsT=w3c[:].bitcast(FP8X4), lhsT_scale=w3s[:], rhs=hc[:].bitcast(FP8X4), rhs_scale=hs[:], start=True, stop=True
+                        out=bank[:, 0:w], lhsT=w3q[0][:].bitcast(FP8X4), lhsT_scale=w3q[1][:], rhs=hc[:].bitcast(FP8X4), rhs_scale=hs[:], start=True, stop=True
                     )
                     res = keep.tile([P, w], F32, name="res%d" % cols.start)
                     if RES_V and cols.stop == U:
@@ -252,6 +291,8 @@ def tile_picked_ydeepm_ent_p_kernel(tc, x_words, x_scales, w1, w2, clm, unit, w3
 
         stages = (position, moves, trades, costs, sums, lookup, utility, hidden)
         for step in range(8 + max(SKEW)):
+            if step == W3_STEP:
+                last_weights()
             for n, stage in enumerate(stages):
                 unit_no = step - SKEW[n]
                 if 0 <= unit_no < 8:

@@ -1,6 +1,7 @@
 from contextlib import ExitStack
 
 import concourse.mybir as mybir
+from concourse.masks import make_identity
 
 F32 = mybir.dt.float32
 BF16 = mybir.dt.bfloat16
@@ -11,289 +12,224 @@ U8 = mybir.dt.uint8
 FP8X4 = mybir.dt.float8_e4m3fn_x4
 ACT = mybir.ActivationFunctionType
 ALU = mybir.AluOpType
-AX = mybir.AxisListType
+AXIS = mybir.AxisListType
 
-P = 128
 K, T, S, D, N, H, V, U = 512, 2048, 1024, 4, 128, 512, 256, 512
-HALF = 512
-CH = 256
 FLOPS = 2 * K * H * S * 2 + 2 * H * N * U
 
-PATH_ON_SCALAR = (1, 2)
-PRV_ON_SCALAR = ((0, 0), (0, 1), (1, 0), (1, 1), (2, 0), (2, 1), (3, 0), (3, 1))
-MODE = "NNNN"
-EVAC_ON_VECTOR = ()
-DL_BUFS = 2
-DS_BUFS = 2
-RING = 4
-LAST_STEPPED = 1
-TAIL = 4
-W1_SPLIT = 1
-SKEW = (0, 1, 3, 3, 3, 6, 6, 7)
-RES_V = 0
-WIDE = (0, 1)
-W3_ON_SCALAR = 0
-W2B_ON_SCALAR = 0
-PER_TILE = 1
-W3_STEP = 2
-SCALE_ON_SCALAR = (0, 1, 2)
+P = 128
+PACK = 4
+LIST_COLUMN = 16
+DATES = S // 2
+PATHS = V // 2
+CLAIMS = U // 2
+COST_RATE = 0.4
+LAST = PACK - 1
+
+SHORT_CHAIN = (0, LAST)
+PATH_TILES_ON_SCALAR = 2
+LOOKUP_LAG = 3
 
 
 def tile_picked_ydeepm_ent_p_kernel(tc, x_words, x_scales, w1, w2, clm, unit, w3, offs, prv, path, out):
     nc = tc.nc
     with ExitStack() as ctx:
-        keep = ctx.enter_context(tc.tile_pool(name="keep", bufs=1))
-        ring = ctx.enter_context(tc.tile_pool(name="ring", bufs=RING))
+        sbuf = ctx.enter_context(tc.tile_pool(name="sbuf", bufs=1))
         psum = ctx.enter_context(tc.psum_pool(name="psum", bufs=1))
 
-        offs_t = keep.tile([P, S // 16], U16, name="offs_t")
-        prv_t = keep.tile([P, S // 16], U16, name="prv_t")
-        path_t = keep.tile([P, U // 16], U16, name="path_t")
-        xw = keep.tile([P, T], U32, name="xw", align_bytes=64)
-        xs = keep.tile([P, T], U8, name="xs", align_bytes=64)
-        w1_cols = H // (1 + W1_SPLIT)
-        w1_raw = [keep.tile([P, 4, w1_cols], F32, name="w1_raw%d" % b) for b in range(1 + W1_SPLIT)]
-        w2_raw = keep.tile([P, 4, H], F32, name="w2_raw")
-        w3_raw = keep.tile([P, 4, N], F32, name="w3_raw")
-        clm_t = keep.tile([P, 4, U], F32, name="clm_t")
-        unit_t = keep.tile([P, 4], F32, name="unit_t")
+        offs_t = sbuf.tile([P, S // LIST_COLUMN], U16, name="offs_t")
+        prv_t = sbuf.tile([P, S // LIST_COLUMN], U16, name="prv_t")
+        path_t = sbuf.tile([P, U // LIST_COLUMN], U16, name="path_t")
+        all_words = sbuf.tile([P, T], U32, name="all_words", align_bytes=64)
+        all_scales = sbuf.tile([P, T], U8, name="all_scales", align_bytes=64)
+        w1_raw = sbuf.tile([P, PACK, H], F32, name="w1_raw")
+        w2_raw = sbuf.tile([P, PACK, H], F32, name="w2_raw")
+        w3_raw = sbuf.tile([P, PACK, N], F32, name="w3_raw")
+        clm_t = sbuf.tile([P, PACK, U], F32, name="clm_t")
+        unit_t = sbuf.tile([P, PACK], F32, name="unit_t")
+        identity = sbuf.tile([P, P], F32, name="identity")
 
         nc.sync.dma_start(offs_t[:], offs)
         for q in range(4):
-            nc.sync.dma_start(xs[32 * q : 32 * q + 32, :].bitcast(I32), x_scales[0, 4 * q : 4 * q + 4, :].bitcast(I32).partition_broadcast(8))
-        nc.sync.dma_start(xw[:].bitcast(I32), x_words[0].rearrange("p n r -> p (n r)").bitcast(I32))
-        for b in range(1 + W1_SPLIT):
-            nc.sync.dma_start(w1_raw[b][:], w1.rearrange("(p j) c -> p j c", j=4)[:, :, w1_cols * b : w1_cols * (b + 1)])
-        nc.sync.dma_start(w2_raw[:], w2.rearrange("(p j) c -> p j c", j=4))
+            rows = x_scales[0, 4 * q : 4 * q + 4, :].bitcast(I32)
+            nc.sync.dma_start(all_scales[32 * q : 32 * q + 32, :].bitcast(I32), rows.partition_broadcast(8))
+        nc.sync.dma_start(all_words[:].bitcast(I32), x_words[0].rearrange("p n r -> p (n r)").bitcast(I32))
+        nc.sync.dma_start(w1_raw[:], w1.rearrange("(p j) c -> p j c", j=PACK))
+        nc.sync.dma_start(w2_raw[:], w2.rearrange("(p j) c -> p j c", j=PACK))
         nc.sync.dma_start(prv_t[:], prv)
-        nc.sync.dma_start(w3_raw[:], w3.rearrange("(p j) c -> p j c", j=4))
+        nc.sync.dma_start(w3_raw[:], w3.rearrange("(p j) c -> p j c", j=PACK))
         nc.sync.dma_start(path_t[:], path)
-        nc.sync.dma_start(unit_t[:], unit.rearrange("(p t) o -> p (t o)", t=4))
-        nc.sync.dma_start(clm_t[:], clm.rearrange("(p t) r -> p t r", t=4))
+        nc.sync.dma_start(unit_t[:], unit.rearrange("(p t) o -> p (t o)", t=PACK))
+        nc.sync.dma_start(clm_t[:], clm.rearrange("(p t) r -> p t r", t=PACK))
+        make_identity(nc, identity[:])
 
-        gs = keep.tile([P, S], U8, name="gs", align_bytes=64)
-        nc.vector.tensor_copy(gs[:], xs[:].indirect(offs_t[:]))
+        def entries(list_tile, cols):
+            return list_tile[:, cols.start // LIST_COLUMN : cols.stop // LIST_COLUMN]
 
-        def deal(wb, raw, a, m0, on_scalar):
-            src = raw[:].rearrange("p j (m t) -> p m j t", t=4)[:, :, :, 2 * a : 2 * a + 2]
-            dst = wb[:].rearrange("p (t m j) -> p m j t", t=2, j=4)[:, m0 : m0 + src.shape[1]]
-            if on_scalar:
-                nc.scalar.copy(dst, src)
-            else:
-                nc.vector.tensor_copy(dst, src)
+        def part(h, width):
+            return slice(width * h, width * (h + 1))
 
-        def quantise(src, width, name):
-            codes = keep.tile([P, width], U32, name=name + "_c", align_bytes=64)
-            scales = keep.tile([P, width], U8, name=name + "_s", align_bytes=64)
-            nc.vector.quantize_mx(out=codes[:].bitcast(FP8X4), scales=scales[:], in_=src)
-            return codes, scales
-
-        gw = [keep.tile([P, HALF], U32, name="gw%d" % h, align_bytes=64) for h in range(2)]
+        picked_scales = sbuf.tile([P, S], U8, name="picked_scales", align_bytes=64)
+        nc.vector.tensor_copy(picked_scales[:], all_scales[:].indirect(offs_t[:]))
+        picked_words = [sbuf.tile([P, DATES], U32, name="picked_words%d" % h, align_bytes=64) for h in range(2)]
         for h in range(2):
-            nc.vector.tensor_copy(gw[h][:], xw[:].indirect(offs_t[:, 32 * h : 32 * h + 32]))
+            nc.vector.tensor_copy(picked_words[h][:], all_words[:].indirect(entries(offs_t, part(h, DATES))))
 
-        w1b = [keep.tile([P, 1024], BF16, name="w1b%d" % a, align_bytes=64) for a in range(2)]
-        w2b = [keep.tile([P, 1024], BF16, name="w2b%d" % a, align_bytes=64) for a in range(2)]
-        if W1_SPLIT:
-            deal(w1b[0], w1_raw[0], 0, 0, True)
-            deal(w1b[1], w1_raw[0], 1, 0, True)
-            deal(w1b[0], w1_raw[1], 0, 64, False)
-            deal(w1b[1], w1_raw[1], 1, 64, True)
-        else:
-            deal(w1b[0], w1_raw[0], 0, 0, False)
-            deal(w1b[1], w1_raw[0], 1, 0, True)
-        w1q = [quantise(w1b[a][:], 256, "w1q%d" % a) for a in range(2)]
-        w2q = []
-        for a in range(2):
-            deal(w2b[a], w2_raw, a, 0, a == 1 and W2B_ON_SCALAR)
-            w2q.append(quantise(w2b[a][:], 256, "w2q%d" % a))
-        w3b = keep.tile([P, N, 4], BF16, name="w3b", align_bytes=64)
-        w3q = []
+        def quantise(values, name):
+            width = values.shape[1] // PACK
+            words = sbuf.tile([P, width], U32, name=name + "_words", align_bytes=64)
+            scales = sbuf.tile([P, width], U8, name=name + "_scales", align_bytes=64)
+            nc.vector.quantize_mx(out=words[:].bitcast(FP8X4), scales=scales[:], in_=values)
+            return words, scales
 
-        def last_weights():
-            dst = w3b[:].rearrange("p (c i) j -> p c j i", i=4)
-            src = w3_raw[:].rearrange("p j (c i) -> p c j i", i=4)
-            if W3_ON_SCALAR:
-                nc.scalar.copy(dst, src)
-            else:
-                nc.vector.tensor_copy(dst, src)
-            w3q.extend(quantise(w3b[:].rearrange("p n j -> p (n j)"), N, "w3q"))
+        def deal(copy, raw, pair, name):
+            dealt = sbuf.tile([P, 2 * P * PACK], BF16, name=name, align_bytes=64)
+            copy(
+                dealt[:].rearrange("p (t m j) -> p m j t", t=2, j=PACK),
+                raw[:].rearrange("p j (m t) -> p m j t", t=PACK)[:, :, :, 2 * pair : 2 * pair + 2],
+            )
+            return dealt
 
-        def product(wq, t, h, bank):
-            codes, scales = wq[t // 2]
-            cols = slice(P * (t % 2), P * (t % 2) + P)
+        w1_dealt = [deal(nc.vector.tensor_copy, w1_raw, 0, "w1_dealt0"), deal(nc.scalar.copy, w1_raw, 1, "w1_dealt1")]
+        w1_mx = [quantise(w1_dealt[pair][:], "w1_%d" % pair) for pair in range(2)]
+        w2_mx = [quantise(deal(nc.vector.tensor_copy, w2_raw, pair, "w2_dealt%d" % pair)[:], "w2_%d" % pair) for pair in range(2)]
+        w3_dealt = sbuf.tile([P, N, PACK], BF16, name="w3_dealt", align_bytes=64)
+        nc.vector.tensor_copy(w3_dealt[:].rearrange("p (c e) j -> p c j e", e=4), w3_raw[:].rearrange("p j (c e) -> p c j e", e=4))
+        w3_words, w3_scales = quantise(w3_dealt[:].rearrange("p n j -> p (n j)"), "w3")
+
+        def product(w_mx, t, h, bank):
+            words, scales = w_mx[t // 2]
+            cols = part(t % 2, P)
             nc.tensor.matmul_mx(
                 out=bank[:],
-                lhsT=codes[:, cols].bitcast(FP8X4),
+                lhsT=words[:, cols].bitcast(FP8X4),
                 lhsT_scale=scales[:, cols],
-                rhs=gw[h][:].bitcast(FP8X4),
-                rhs_scale=gs[:, HALF * h : HALF * h + HALF],
+                rhs=picked_words[h][:].bitcast(FP8X4),
+                rhs_scale=picked_scales[:, part(h, DATES)],
                 start=True,
                 stop=True,
             )
 
-        pos = [keep.tile([P, S], F32, name="pos%d" % t) for t in range(4)]
-        term = [keep.tile([P, 3 * V if MODE[t] in "NA" else 2 * V], F32, name="term%d" % t) for t in range(4)]
-        hb = keep.tile([P, 4, U], BF16, name="hb")
-        hq = keep.tile([P, U, 4], BF16, name="hq", align_bytes=64)
-        twin, loss, diff, cost, back, spent, net, eu, th, tpp = {}, {}, {}, {}, {}, {}, {}, {}, {}, {}
+        pos = [sbuf.tile([P, S], F32, name="pos%d" % t) for t in range(PACK)]
+        owed = [sbuf.tile([P, 2 * V], F32, name="owed%d" % t) for t in range(PACK)]
+        owed_bank, traded, pos_copy, loss, trade, cost = {}, {}, {}, {}, {}, {}
+        net = [sbuf.tile([P, U], F32, name="net%d" % t) for t in range(PACK)]
+        looked_up = [sbuf.tile([P, U], F32, name="looked_up%d" % t) for t in range(PATH_TILES_ON_SCALAR)]
+        bounded = [sbuf.tile([P, U], F32, name="bounded%d" % t) for t in range(PACK)]
+        eu = [sbuf.tile([P, U], F32, name="eu%d" % t) for t in range(PACK)]
+        hid_rows = sbuf.tile([P, LAST, U], BF16, name="hid_rows")
+        hid = sbuf.tile([P, U, PACK], BF16, name="hid", align_bytes=64)
 
-        def half(h):
-            return slice(HALF * h, HALF * h + HALF)
+        def positions(t, h):
+            bank = psum.tile([P, DATES], F32, name="bank", tag="dl_and_out", bufs=3)
+            product(w1_mx, t, h, bank)
+            nc.scalar.activation(pos[t][:, part(h, DATES)], bank[:], ACT.Tanh)
+            if h == 1:
+                pos_copy[t] = sbuf.tile([P, DATES], F32, name="pos_copy%d" % t)
+                nc.sync.dma_start(pos_copy[t][:], pos[t][:, part(h, DATES)])
 
-        def chunks(t, c):
-            if t in WIDE and MODE[t] in "NA":
-                return [slice(0, U)] if c == 0 else []
-            n = TAIL // 2 if t == 3 else 1
-            w = CH // n
-            return [slice(CH * c + w * k, CH * c + w * k + w) for k in range(n)]
-
-        def leave(t, dst, bank):
-            if t in EVAC_ON_VECTOR:
-                nc.vector.tensor_copy(dst, bank)
-            else:
-                nc.scalar.copy(dst, bank)
-
-        def position(t, h):
-            bank = psum.tile([P, HALF], F32, name="dl", tag="dl", bufs=DL_BUFS)
-            product(w1q, t, h, bank)
-            nc.scalar.activation(pos[t][:, half(h)], bank[:], ACT.Tanh)
-            if (t, h) not in PRV_ON_SCALAR:
-                twin[t, h] = keep.tile([P, HALF], F32, name="twin%d_%d" % (t, h))
-                nc.sync.dma_start(twin[t, h][:], pos[t][:, half(h)])
-
-        def moves(t, h):
-            bank = psum.tile([P, HALF], F32, name="ds", tag="ds", bufs=DS_BUFS)
-            product(w2q, t, h, bank)
-            if MODE[t] in "NA":
-                loss[t, h] = ring.tile([P, HALF], F32, name="loss")
-                nc.vector.scalar_tensor_tensor(loss[t, h][:], bank[:], -1.0, pos[t][:, half(h)], ALU.mult, ALU.mult)
-                return
-            loss[t, h] = ring.tile([P, D, P], F32, name="loss")
+        def losses(t, h):
+            bank = psum.tile([P, DATES], F32, name="bank", tag="ds", bufs=2)
+            product(w2_mx, t, h, bank)
+            loss[t, h] = sbuf.tile([P, D, PATHS], F32, name="loss%d_%d" % (t, h))
             nc.vector.scalar_tensor_tensor(
                 loss[t, h][:].rearrange("p d v -> p v d"),
                 bank[:].rearrange("p (v d) -> p v d", d=D),
                 -1.0,
-                pos[t][:, half(h)].rearrange("p (v d) -> p v d", d=D),
+                pos[t][:, part(h, DATES)].rearrange("p (v d) -> p v d", d=D),
                 ALU.mult,
                 ALU.mult,
             )
 
         def trades(t, h):
-            diff[t, h] = ring.tile([P, HALF], F32, name="diff")
-            looked = pos[t][:].indirect(prv_t[:, 32 * h : 32 * h + 32])
-            if (t, h) in PRV_ON_SCALAR:
-                dp = ring.tile([P, HALF], F32, name="dp")
-                nc.scalar.activation(dp[:], looked, ACT.Copy)
-                nc.vector.tensor_tensor(diff[t, h][:], dp[:], pos[t][:, half(h)], ALU.subtract)
+            trade[t, h] = sbuf.tile([P, DATES], F32, name="trade%d_%d" % (t, h))
+            at_prv = pos[t][:].indirect(entries(prv_t, part(h, DATES)))
+            if h == 0:
+                dp = sbuf.tile([P, DATES], F32, name="dp%d" % t)
+                nc.scalar.activation(dp[:], at_prv, ACT.Copy)
+                nc.vector.tensor_tensor(trade[t, h][:], dp[:], pos[t][:, part(h, DATES)], ALU.subtract)
             else:
-                nc.vector.tensor_tensor(diff[t, h][:], looked, twin[t, h][:], ALU.subtract)
+                nc.vector.tensor_tensor(trade[t, h][:], at_prv, pos_copy[t][:], ALU.subtract)
 
         def costs(t, h):
-            grouped = diff[t, h][:].rearrange("p (v d) -> p v d", d=D)
-            if MODE[t] == "A":
-                cost[t, h] = ring.tile([P, HALF], F32, name="cost")
-                nc.scalar.activation(cost[t, h][:], diff[t, h][:], ACT.Abs, scale=0.4)
-            elif MODE[t] in "RN":
+            by_path = trade[t, h][:].rearrange("p (v d) -> p v d", d=D)
+            if t in SHORT_CHAIN:
                 if h == 0:
-                    spent[t] = keep.tile([P, V], F32, name="spent%d" % t)
-                nc.vector.tensor_reduce(spent[t][:, P * h : P * h + P], grouped, AX.X, ALU.add, apply_absolute_value=True)
+                    traded[t] = sbuf.tile([P, V], F32, name="traded%d" % t)
+                nc.vector.tensor_reduce(traded[t][:, part(h, PATHS)], by_path, AXIS.X, ALU.add, apply_absolute_value=True)
             else:
-                cost[t, h] = ring.tile([P, D, P], F32, name="cost")
-                nc.scalar.activation(cost[t, h][:].rearrange("p d v -> p v d"), grouped, ACT.Abs, scale=0.4)
+                cost[t, h] = sbuf.tile([P, D, PATHS], F32, name="cost%d_%d" % (t, h))
+                nc.scalar.activation(cost[t, h][:].rearrange("p d v -> p v d"), by_path, ACT.Abs, scale=COST_RATE)
 
         def sums(t, h):
-            if MODE[t] in "NA":
-                src = loss[t, h]
-                if MODE[t] == "A":
-                    src = ring.tile([P, HALF], F32, name="pnl")
-                    nc.vector.tensor_tensor(src[:], loss[t, h][:], cost[t, h][:], ALU.add)
-                grouped = src[:].rearrange("p (v d) -> p v d", d=D)
-                pairs = term[t][:, V : 3 * V].rearrange("p (v e) -> p v e", e=2)
-                nc.vector.tensor_tensor(pairs[:, P * h : P * h + P, :], grouped[:, :, 0:2], grouped[:, :, 2:4], ALU.add)
-                if PER_TILE and h == 0:
-                    return
-                vs = slice(0, V) if PER_TILE else slice(P * h, P * h + P)
-                first = pairs[:, vs, 0]
-                if MODE[t] == "N":
-                    part = ring.tile([P, V], F32, name="part")
-                    nc.vector.scalar_tensor_tensor(part[:, vs], spent[t][:, vs], 0.4, first, ALU.mult, ALU.add)
-                    first = part[:, vs]
-                nc.vector.tensor_tensor(term[t][:, vs], first, pairs[:, vs, 1], ALU.add)
-                return
-            parts = [loss[t, h][:, d, :] for d in range(D)]
-            if MODE[t] == "P":
-                parts = parts + [cost[t, h][:, d, :] for d in range(D)]
-            bank = psum.tile([P, P], F32, name="sums", tag="sums", bufs=2)
-            for n, part in enumerate(parts):
-                nc.tensor.matmul(bank[:], lhsT=part, rhs=None, is_transpose=True, start=(n == 0), stop=(n == len(parts) - 1))
-            turned = term[t][:, V + P * h : V + P * h + P]
-            leave(t, turned, bank[:])
+            summands = [loss[t, h][:, d, :] for d in range(D)]
+            if t not in SHORT_CHAIN:
+                summands = summands + [cost[t, h][:, d, :] for d in range(D)]
+            bank = psum.tile([P, P], F32, name="bank", tag="turned_sums", bufs=2)
+            for n, summand in enumerate(summands):
+                nc.tensor.matmul(bank[:], lhsT=summand, rhs=identity[:], is_transpose=True, start=(n == 0), stop=(n == len(summands) - 1))
+            turned = owed[t][:, V + PATHS * h : V + PATHS * (h + 1)]
+            nc.scalar.copy(turned, bank[:])
             if h == 0:
-                back[t] = psum.tile([P, V], F32, name="back", tag="back", bufs=1)
-            nc.tensor.transpose(back[t][:, P * h : P * h + P], turned, None)
+                owed_bank[t] = psum.tile([P, V], F32, name="owed_bank", tag="owed", bufs=1)
+            nc.tensor.transpose(owed_bank[t][:, part(h, PATHS)], turned, identity[:])
             if h == 1:
-                if MODE[t] == "R":
-                    nc.vector.scalar_tensor_tensor(term[t][:, 0:V], spent[t][:], 0.4, back[t][:], ALU.mult, ALU.add)
+                if t in SHORT_CHAIN:
+                    nc.vector.scalar_tensor_tensor(owed[t][:, 0:V], traded[t][:], COST_RATE, owed_bank[t][:], ALU.mult, ALU.add)
                 else:
-                    leave(t, term[t][:, 0:V], back[t][:])
+                    nc.scalar.copy(owed[t][:, 0:V], owed_bank[t][:])
 
-        def lookup(t, c):
-            if c == 0:
-                net[t] = keep.tile([P, U], F32, name="net%d" % t)
-                tpp[t] = keep.tile([P, U], F32, name="tpp%d" % t)
-            for cols in chunks(t, c):
-                looked = term[t][:].indirect(path_t[:, cols.start // 16 : cols.stop // 16])
-                if t in PATH_ON_SCALAR:
-                    nc.scalar.activation(tpp[t][:, cols], looked, ACT.Copy)
-                    nc.vector.tensor_tensor(net[t][:, cols], tpp[t][:, cols], clm_t[:, t, cols], ALU.add)
-                else:
-                    nc.vector.tensor_tensor(net[t][:, cols], looked, clm_t[:, t, cols], ALU.add)
+        def lookups(t, h):
+            cols = part(h, CLAIMS)
+            at_path = owed[t][:].indirect(entries(path_t, cols))
+            if t < PATH_TILES_ON_SCALAR:
+                nc.scalar.activation(looked_up[t][:, cols], at_path, ACT.Copy)
+                nc.vector.tensor_tensor(net[t][:, cols], looked_up[t][:, cols], clm_t[:, t, cols], ALU.add)
+            else:
+                nc.vector.tensor_tensor(net[t][:, cols], at_path, clm_t[:, t, cols], ALU.add)
 
-        def utility(t, c):
-            if c == 0:
-                th[t] = keep.tile([P, U], F32, name="th%d" % t)
-                eu[t] = keep.tile([P, U], F32, name="eu%d" % t)
-            for cols in chunks(t, c):
-                nc.scalar.activation(th[t][:, cols], net[t][:, cols], ACT.Tanh)
-                nc.scalar.activation(eu[t][:, cols], th[t][:, cols], ACT.Exp)
+        def utilities(t, h):
+            cols = part(h, CLAIMS)
+            nc.scalar.activation(bounded[t][:, cols], net[t][:, cols], ACT.Tanh)
+            nc.scalar.activation(eu[t][:, cols], bounded[t][:, cols], ACT.Exp)
 
-        def weave(cols, tiles):
-            nc.vector.tensor_copy(
-                hq[:, cols, 0:tiles].rearrange("p (c i) t -> p c t i", i=4), hb[:, 0:tiles, cols].rearrange("p t (c i) -> p c t i", i=4)
-            )
+        def hidden(t, h):
+            cols = part(h, CLAIMS)
+            target = hid[:, cols, t] if t == LAST else hid_rows[:, t, cols]
+            nc.vector.tensor_scalar(target, eu[t][:, cols], unit_t[:, t : t + 1], None, ALU.mult)
+            if t == LAST - 1:
+                nc.vector.tensor_copy(
+                    hid[:, cols, 0:LAST].rearrange("p (c e) t -> p c t e", e=4),
+                    hid_rows[:, :, cols].rearrange("p t (c e) -> p c t e", e=4),
+                )
+            if t == LAST:
+                hid_words, hid_scales = quantise(hid[:, cols, :].rearrange("p r t -> p (r t)"), "hid%d" % h)
+                bank = psum.tile([P, DATES], F32, name="bank", tag="dl_and_out", bufs=3)
+                nc.tensor.matmul_mx(
+                    out=bank[:, 0:CLAIMS],
+                    lhsT=w3_words[:].bitcast(FP8X4),
+                    lhsT_scale=w3_scales[:],
+                    rhs=hid_words[:].bitcast(FP8X4),
+                    rhs_scale=hid_scales[:],
+                    start=True,
+                    stop=True,
+                )
+                result = sbuf.tile([P, CLAIMS], F32, name="result%d" % h)
+                nc.scalar.copy(result[:], bank[:, 0:CLAIMS])
+                nc.sync.dma_start(out[:, cols], result[:])
 
-        def hidden(t, c):
-            for cols in chunks(t, c):
-                if LAST_STEPPED and t == 3:
-                    nc.vector.tensor_scalar(hq[:, cols, t], eu[t][:, cols], unit_t[:, t : t + 1], None, ALU.mult)
-                elif t in SCALE_ON_SCALAR:
-                    nc.scalar.activation(hb[:, t, cols], eu[t][:, cols], ACT.Copy, scale=unit_t[:, t : t + 1])
-                else:
-                    nc.vector.tensor_scalar(hb[:, t, cols], eu[t][:, cols], unit_t[:, t : t + 1], None, ALU.mult)
-                if LAST_STEPPED and t == 2:
-                    weave(cols, 3)
-                if t == 3:
-                    if not LAST_STEPPED:
-                        weave(cols, 4)
-                    w = cols.stop - cols.start
-                    hc, hs = quantise(hq[:, cols, :].rearrange("p r t -> p (r t)"), w, "hq%d" % cols.start)
-                    bank = psum.tile([P, HALF], F32, name="dl", tag="dl", bufs=DL_BUFS)
-                    nc.tensor.matmul_mx(
-                        out=bank[:, 0:w], lhsT=w3q[0][:].bitcast(FP8X4), lhsT_scale=w3q[1][:], rhs=hc[:].bitcast(FP8X4), rhs_scale=hs[:], start=True, stop=True
-                    )
-                    res = keep.tile([P, w], F32, name="res%d" % cols.start)
-                    if RES_V and cols.stop == U:
-                        nc.vector.tensor_copy(res[:], bank[:, 0:w])
-                    else:
-                        nc.scalar.copy(res[:], bank[:, 0:w])
-                    nc.sync.dma_start(out[:, cols], res[:])
-
-        stages = (position, moves, trades, costs, sums, lookup, utility, hidden)
-        for step in range(8 + max(SKEW)):
-            if step == W3_STEP:
-                last_weights()
-            for n, stage in enumerate(stages):
-                unit_no = step - SKEW[n]
-                if 0 <= unit_no < 8:
-                    stage(unit_no // 2, unit_no % 2)
+        lags = (
+            (positions, 0),
+            (losses, 1),
+            (trades, 1),
+            (costs, 2),
+            (sums, 3),
+            (lookups, 3 + LOOKUP_LAG),
+            (utilities, 4 + LOOKUP_LAG),
+            (hidden, 5 + LOOKUP_LAG),
+        )
+        halves = 2 * PACK
+        for step in range(halves + lags[-1][1]):
+            for stage, lag in lags:
+                if 0 <= step - lag < halves:
+                    stage(*divmod(step - lag, 2))

@@ -69,6 +69,11 @@ def tile_picked_ydeepm_ent_p_kernel(tc, x_words, x_scales, w1, w2, clm, unit, w3
         def part(h, width):
             return slice(width * h, width * (h + 1))
 
+        def claim_pieces(t, h):
+            pieces = 2 if (t, h) == (LAST, 1) else 1
+            width = CLAIMS // pieces
+            return [part(pieces * h + n, width) for n in range(pieces)]
+
         picked_scales = sbuf.tile([P, S], U8, name="picked_scales", align_bytes=64)
         nc.vector.tensor_copy(picked_scales[:], all_scales[:].indirect(offs_t[:]))
         picked_words = [sbuf.tile([P, DATES], U32, name="picked_words%d" % h, align_bytes=64) for h in range(2)]
@@ -180,43 +185,50 @@ def tile_picked_ydeepm_ent_p_kernel(tc, x_words, x_scales, w1, w2, clm, unit, w3
                     nc.scalar.copy(owed[t][:, 0:V], owed_bank[t][:])
 
         def lookups(t, h):
-            cols = part(h, CLAIMS)
-            at_path = owed[t][:].indirect(entries(path_t, cols))
-            if t < PATH_TILES_ON_SCALAR:
-                nc.scalar.activation(looked_up[t][:, cols], at_path, ACT.Copy)
-                nc.vector.tensor_tensor(net[t][:, cols], looked_up[t][:, cols], clm_t[:, t, cols], ALU.add)
-            else:
-                nc.vector.tensor_tensor(net[t][:, cols], at_path, clm_t[:, t, cols], ALU.add)
+            for cols in claim_pieces(t, h):
+                at_path = owed[t][:].indirect(entries(path_t, cols))
+                if t < PATH_TILES_ON_SCALAR:
+                    nc.scalar.activation(looked_up[t][:, cols], at_path, ACT.Copy)
+                    nc.vector.tensor_tensor(net[t][:, cols], looked_up[t][:, cols], clm_t[:, t, cols], ALU.add)
+                else:
+                    nc.vector.tensor_tensor(net[t][:, cols], at_path, clm_t[:, t, cols], ALU.add)
 
         def utilities(t, h):
-            cols = part(h, CLAIMS)
-            nc.scalar.activation(bounded[t][:, cols], net[t][:, cols], ACT.Tanh)
-            nc.scalar.activation(eu[t][:, cols], bounded[t][:, cols], ACT.Exp)
+            for cols in claim_pieces(t, h):
+                nc.scalar.activation(bounded[t][:, cols], net[t][:, cols], ACT.Tanh)
+                nc.scalar.activation(eu[t][:, cols], bounded[t][:, cols], ACT.Exp)
 
         def hidden(t, h):
-            cols = part(h, CLAIMS)
-            target = hid[:, cols, t] if t == LAST else hid_rows[:, t, cols]
-            nc.vector.tensor_scalar(target, eu[t][:, cols], unit_t[:, t : t + 1], None, ALU.mult)
-            if t == LAST - 1:
-                nc.vector.tensor_copy(
-                    hid[:, cols, 0:LAST].rearrange("p (c e) t -> p c t e", e=4),
-                    hid_rows[:, :, cols].rearrange("p t (c e) -> p c t e", e=4),
-                )
-            if t == LAST:
-                hid_words, hid_scales = quantise(hid[:, cols, :].rearrange("p r t -> p (r t)"), "hid%d" % h)
-                bank = psum.tile([P, DATES], F32, name="bank", tag="dl_and_out", bufs=3)
-                nc.tensor.matmul_mx(
-                    out=bank[:, 0:CLAIMS],
-                    lhsT=w3_words[:].bitcast(FP8X4),
-                    lhsT_scale=w3_scales[:],
-                    rhs=hid_words[:].bitcast(FP8X4),
-                    rhs_scale=hid_scales[:],
-                    start=True,
-                    stop=True,
-                )
-                result = sbuf.tile([P, CLAIMS], F32, name="result%d" % h)
-                nc.scalar.copy(result[:], bank[:, 0:CLAIMS])
-                nc.sync.dma_start(out[:, cols], result[:])
+            factor = unit_t[:, t : t + 1]
+            for cols in claim_pieces(t, h):
+                if t == LAST:
+                    nc.vector.tensor_scalar(hid[:, cols, t], eu[t][:, cols], factor, None, ALU.mult)
+                    risk_factors(cols)
+                elif t == LAST - 1:
+                    nc.scalar.activation(hid_rows[:, t, cols], eu[t][:, cols], ACT.Copy, scale=factor)
+                    nc.vector.tensor_copy(
+                        hid[:, cols, 0:LAST].rearrange("p (c e) t -> p c t e", e=4),
+                        hid_rows[:, :, cols].rearrange("p t (c e) -> p c t e", e=4),
+                    )
+                else:
+                    nc.vector.tensor_scalar(hid_rows[:, t, cols], eu[t][:, cols], factor, None, ALU.mult)
+
+        def risk_factors(cols):
+            width = cols.stop - cols.start
+            hid_words, hid_scales = quantise(hid[:, cols, :].rearrange("p r t -> p (r t)"), "hid%d" % cols.start)
+            bank = psum.tile([P, DATES], F32, name="bank", tag="dl_and_out", bufs=3)
+            nc.tensor.matmul_mx(
+                out=bank[:, 0:width],
+                lhsT=w3_words[:].bitcast(FP8X4),
+                lhsT_scale=w3_scales[:],
+                rhs=hid_words[:].bitcast(FP8X4),
+                rhs_scale=hid_scales[:],
+                start=True,
+                stop=True,
+            )
+            result = sbuf.tile([P, width], F32, name="result%d" % cols.start)
+            nc.scalar.copy(result[:], bank[:, 0:width])
+            nc.sync.dma_start(out[:, cols], result[:])
 
         lags = (
             (positions, 0),

from contextlib import ExitStack

import concourse.mybir as mybir
from concourse.masks import make_identity

F32 = mybir.dt.float32
BF16 = mybir.dt.bfloat16
I32 = mybir.dt.int32
U32 = mybir.dt.uint32
U16 = mybir.dt.uint16
U8 = mybir.dt.uint8
FP8X4 = mybir.dt.float8_e4m3fn_x4
ACT = mybir.ActivationFunctionType
ALU = mybir.AluOpType
AXIS = mybir.AxisListType

K, T, S, D, N, H, V, U = 512, 2048, 1024, 4, 128, 512, 256, 512
FLOPS = 2 * K * H * S * 2 + 2 * H * N * U

P = 128
PACK = 4
LIST_COLUMN = 16
DATES = S // 2
PATHS = V // 2
CLAIMS = U // 2
COST_RATE = 0.4
LAST = PACK - 1

SHORT_CHAIN = (0, LAST)
PATH_TILES_ON_SCALAR = 2
LOOKUP_LAG = 3


def tile_picked_ydeepm_ent_p_kernel(tc, x_words, x_scales, w1, w2, clm, unit, w3, offs, prv, path, out):
    nc = tc.nc
    with ExitStack() as ctx:
        sbuf = ctx.enter_context(tc.tile_pool(name="sbuf", bufs=1))
        psum = ctx.enter_context(tc.psum_pool(name="psum", bufs=1))

        offs_t = sbuf.tile([P, S // LIST_COLUMN], U16, name="offs_t")
        prv_t = sbuf.tile([P, S // LIST_COLUMN], U16, name="prv_t")
        path_t = sbuf.tile([P, U // LIST_COLUMN], U16, name="path_t")
        all_words = sbuf.tile([P, T], U32, name="all_words", align_bytes=64)
        all_scales = sbuf.tile([P, T], U8, name="all_scales", align_bytes=64)
        w1_raw = sbuf.tile([P, PACK, H], F32, name="w1_raw")
        w2_raw = sbuf.tile([P, PACK, H], F32, name="w2_raw")
        w3_raw = sbuf.tile([P, PACK, N], F32, name="w3_raw")
        clm_t = sbuf.tile([P, PACK, U], F32, name="clm_t")
        unit_t = sbuf.tile([P, PACK], F32, name="unit_t")
        identity = sbuf.tile([P, P], F32, name="identity")

        nc.sync.dma_start(offs_t[:], offs)
        for q in range(4):
            rows = x_scales[0, 4 * q : 4 * q + 4, :].bitcast(I32)
            nc.sync.dma_start(all_scales[32 * q : 32 * q + 32, :].bitcast(I32), rows.partition_broadcast(8))
        nc.sync.dma_start(all_words[:].bitcast(I32), x_words[0].rearrange("p n r -> p (n r)").bitcast(I32))
        nc.sync.dma_start(w1_raw[:], w1.rearrange("(p j) c -> p j c", j=PACK))
        nc.sync.dma_start(w2_raw[:], w2.rearrange("(p j) c -> p j c", j=PACK))
        nc.sync.dma_start(prv_t[:], prv)
        nc.sync.dma_start(w3_raw[:], w3.rearrange("(p j) c -> p j c", j=PACK))
        nc.sync.dma_start(path_t[:], path)
        nc.sync.dma_start(unit_t[:], unit.rearrange("(p t) o -> p (t o)", t=PACK))
        nc.sync.dma_start(clm_t[:], clm.rearrange("(p t) r -> p t r", t=PACK))
        make_identity(nc, identity[:])

        def entries(list_tile, cols):
            return list_tile[:, cols.start // LIST_COLUMN : cols.stop // LIST_COLUMN]

        def part(h, width):
            return slice(width * h, width * (h + 1))

        def claim_pieces(t, h):
            pieces = 2 if (t, h) == (LAST, 1) else 1
            width = CLAIMS // pieces
            return [part(pieces * h + n, width) for n in range(pieces)]

        picked_scales = sbuf.tile([P, S], U8, name="picked_scales", align_bytes=64)
        nc.vector.tensor_copy(picked_scales[:], all_scales[:].indirect(offs_t[:]))
        picked_words = [sbuf.tile([P, DATES], U32, name="picked_words%d" % h, align_bytes=64) for h in range(2)]
        for h in range(2):
            nc.vector.tensor_copy(picked_words[h][:], all_words[:].indirect(entries(offs_t, part(h, DATES))))

        def quantise(values, name):
            width = values.shape[1] // PACK
            words = sbuf.tile([P, width], U32, name=name + "_words", align_bytes=64)
            scales = sbuf.tile([P, width], U8, name=name + "_scales", align_bytes=64)
            nc.vector.quantize_mx(out=words[:].bitcast(FP8X4), scales=scales[:], in_=values)
            return words, scales

        def deal(copy, raw, pair, name):
            dealt = sbuf.tile([P, 2 * P * PACK], BF16, name=name, align_bytes=64)
            copy(
                dealt[:].rearrange("p (t m j) -> p m j t", t=2, j=PACK),
                raw[:].rearrange("p j (m t) -> p m j t", t=PACK)[:, :, :, 2 * pair : 2 * pair + 2],
            )
            return dealt

        w1_dealt = [deal(nc.vector.tensor_copy, w1_raw, 0, "w1_dealt0"), deal(nc.scalar.copy, w1_raw, 1, "w1_dealt1")]
        w1_mx = [quantise(w1_dealt[pair][:], "w1_%d" % pair) for pair in range(2)]
        w2_mx = [quantise(deal(nc.vector.tensor_copy, w2_raw, pair, "w2_dealt%d" % pair)[:], "w2_%d" % pair) for pair in range(2)]
        w3_dealt = sbuf.tile([P, N, PACK], BF16, name="w3_dealt", align_bytes=64)
        nc.vector.tensor_copy(w3_dealt[:].rearrange("p (c e) j -> p c j e", e=4), w3_raw[:].rearrange("p j (c e) -> p c j e", e=4))
        w3_words, w3_scales = quantise(w3_dealt[:].rearrange("p n j -> p (n j)"), "w3")

        def product(w_mx, t, h, bank):
            words, scales = w_mx[t // 2]
            cols = part(t % 2, P)
            nc.tensor.matmul_mx(
                out=bank[:],
                lhsT=words[:, cols].bitcast(FP8X4),
                lhsT_scale=scales[:, cols],
                rhs=picked_words[h][:].bitcast(FP8X4),
                rhs_scale=picked_scales[:, part(h, DATES)],
                start=True,
                stop=True,
            )

        pos = [sbuf.tile([P, S], F32, name="pos%d" % t) for t in range(PACK)]
        owed = [sbuf.tile([P, 2 * V], F32, name="owed%d" % t) for t in range(PACK)]
        owed_bank, traded, pos_copy, loss, trade, cost = {}, {}, {}, {}, {}, {}
        net = [sbuf.tile([P, U], F32, name="net%d" % t) for t in range(PACK)]
        looked_up = [sbuf.tile([P, U], F32, name="looked_up%d" % t) for t in range(PATH_TILES_ON_SCALAR)]
        bounded = [sbuf.tile([P, U], F32, name="bounded%d" % t) for t in range(PACK)]
        eu = [sbuf.tile([P, U], F32, name="eu%d" % t) for t in range(PACK)]
        hid_rows = sbuf.tile([P, LAST, U], BF16, name="hid_rows")
        hid = sbuf.tile([P, U, PACK], BF16, name="hid", align_bytes=64)

        def positions(t, h):
            bank = psum.tile([P, DATES], F32, name="bank", tag="dl_and_out", bufs=3)
            product(w1_mx, t, h, bank)
            nc.scalar.activation(pos[t][:, part(h, DATES)], bank[:], ACT.Tanh)
            if h == 1:
                pos_copy[t] = sbuf.tile([P, DATES], F32, name="pos_copy%d" % t)
                nc.sync.dma_start(pos_copy[t][:], pos[t][:, part(h, DATES)])

        def losses(t, h):
            bank = psum.tile([P, DATES], F32, name="bank", tag="ds", bufs=2)
            product(w2_mx, t, h, bank)
            loss[t, h] = sbuf.tile([P, D, PATHS], F32, name="loss%d_%d" % (t, h))
            nc.vector.scalar_tensor_tensor(
                loss[t, h][:].rearrange("p d v -> p v d"),
                bank[:].rearrange("p (v d) -> p v d", d=D),
                -1.0,
                pos[t][:, part(h, DATES)].rearrange("p (v d) -> p v d", d=D),
                ALU.mult,
                ALU.mult,
            )

        def trades(t, h):
            trade[t, h] = sbuf.tile([P, DATES], F32, name="trade%d_%d" % (t, h))
            at_prv = pos[t][:].indirect(entries(prv_t, part(h, DATES)))
            if h == 0:
                dp = sbuf.tile([P, DATES], F32, name="dp%d" % t)
                nc.scalar.activation(dp[:], at_prv, ACT.Copy)
                nc.vector.tensor_tensor(trade[t, h][:], dp[:], pos[t][:, part(h, DATES)], ALU.subtract)
            else:
                nc.vector.tensor_tensor(trade[t, h][:], at_prv, pos_copy[t][:], ALU.subtract)

        def costs(t, h):
            by_path = trade[t, h][:].rearrange("p (v d) -> p v d", d=D)
            if t in SHORT_CHAIN:
                if h == 0:
                    traded[t] = sbuf.tile([P, V], F32, name="traded%d" % t)
                nc.vector.tensor_reduce(traded[t][:, part(h, PATHS)], by_path, AXIS.X, ALU.add, apply_absolute_value=True)
            else:
                cost[t, h] = sbuf.tile([P, D, PATHS], F32, name="cost%d_%d" % (t, h))
                nc.scalar.activation(cost[t, h][:].rearrange("p d v -> p v d"), by_path, ACT.Abs, scale=COST_RATE)

        def sums(t, h):
            summands = [loss[t, h][:, d, :] for d in range(D)]
            if t not in SHORT_CHAIN:
                summands = summands + [cost[t, h][:, d, :] for d in range(D)]
            bank = psum.tile([P, P], F32, name="bank", tag="turned_sums", bufs=2)
            for n, summand in enumerate(summands):
                nc.tensor.matmul(bank[:], lhsT=summand, rhs=identity[:], is_transpose=True, start=(n == 0), stop=(n == len(summands) - 1))
            turned = owed[t][:, V + PATHS * h : V + PATHS * (h + 1)]
            nc.scalar.copy(turned, bank[:])
            if h == 0:
                owed_bank[t] = psum.tile([P, V], F32, name="owed_bank", tag="owed", bufs=1)
            nc.tensor.transpose(owed_bank[t][:, part(h, PATHS)], turned, identity[:])
            if h == 1:
                if t in SHORT_CHAIN:
                    nc.vector.scalar_tensor_tensor(owed[t][:, 0:V], traded[t][:], COST_RATE, owed_bank[t][:], ALU.mult, ALU.add)
                else:
                    nc.scalar.copy(owed[t][:, 0:V], owed_bank[t][:])

        def lookups(t, h):
            for cols in claim_pieces(t, h):
                at_path = owed[t][:].indirect(entries(path_t, cols))
                if t < PATH_TILES_ON_SCALAR:
                    nc.scalar.activation(looked_up[t][:, cols], at_path, ACT.Copy)
                    nc.vector.tensor_tensor(net[t][:, cols], looked_up[t][:, cols], clm_t[:, t, cols], ALU.add)
                else:
                    nc.vector.tensor_tensor(net[t][:, cols], at_path, clm_t[:, t, cols], ALU.add)

        def utilities(t, h):
            for cols in claim_pieces(t, h):
                nc.scalar.activation(bounded[t][:, cols], net[t][:, cols], ACT.Tanh)
                nc.scalar.activation(eu[t][:, cols], bounded[t][:, cols], ACT.Exp)

        def hidden(t, h):
            factor = unit_t[:, t : t + 1]
            for cols in claim_pieces(t, h):
                if t == LAST:
                    nc.vector.tensor_scalar(hid[:, cols, t], eu[t][:, cols], factor, None, ALU.mult)
                    risk_factors(cols)
                elif t == LAST - 1:
                    nc.scalar.activation(hid_rows[:, t, cols], eu[t][:, cols], ACT.Copy, scale=factor)
                    nc.vector.tensor_copy(
                        hid[:, cols, 0:LAST].rearrange("p (c e) t -> p c t e", e=4),
                        hid_rows[:, :, cols].rearrange("p t (c e) -> p c t e", e=4),
                    )
                else:
                    nc.vector.tensor_scalar(hid_rows[:, t, cols], eu[t][:, cols], factor, None, ALU.mult)

        def risk_factors(cols):
            width = cols.stop - cols.start
            hid_words, hid_scales = quantise(hid[:, cols, :].rearrange("p r t -> p (r t)"), "hid%d" % cols.start)
            bank = psum.tile([P, DATES], F32, name="bank", tag="dl_and_out", bufs=3)
            nc.tensor.matmul_mx(
                out=bank[:, 0:width],
                lhsT=w3_words[:].bitcast(FP8X4),
                lhsT_scale=w3_scales[:],
                rhs=hid_words[:].bitcast(FP8X4),
                rhs_scale=hid_scales[:],
                start=True,
                stop=True,
            )
            result = sbuf.tile([P, width], F32, name="result%d" % cols.start)
            nc.scalar.copy(result[:], bank[:, 0:width])
            nc.sync.dma_start(out[:, cols], result[:])

        lags = (
            (positions, 0),
            (losses, 1),
            (trades, 1),
            (costs, 2),
            (sums, 3),
            (lookups, 3 + LOOKUP_LAG),
            (utilities, 4 + LOOKUP_LAG),
            (hidden, 5 + LOOKUP_LAG),
        )
        halves = 2 * PACK
        for step in range(halves + lags[-1][1]):
            for stage, lag in lags:
                if 0 <= step - lag < halves:
                    stage(*divmod(step - lag, 2))
